import numpy as np, ml_dtypes
CORES = [8,9,10,11,12,13]
N = 6
import mx_ref
BF = ml_dtypes.bfloat16
def gentries(a):
    return np.ascontiguousarray(a.reshape(8, 16, -1).transpose(0, 2, 1)).reshape(8, -1)
def gtable(e):
    e = np.asarray(e); return np.ascontiguousarray(e.reshape(8, -1, 16).transpose(0, 2, 1)).reshape(128, -1).astype(np.int32)
def gcols(t, e):
    v = np.concatenate([t.reshape(8, 16, -1, 4), np.zeros((8, 16, 1, 4), BF)], axis=2)
    return np.ascontiguousarray(np.stack([v[g][:, e[g]] for g in range(8)])).reshape(128, -1)
def f(rng, *shape):
    return mx_ref.flush((rng.standard_normal(shape, dtype=np.float32) * np.exp2(rng.integers(-2, 3, shape[:-1] + (1,)))).astype(BF))
def wide(rng, *shape, cols=0):
    v = rng.standard_normal(shape, dtype=np.float32) * np.exp2(rng.integers(-12, 13, shape)).astype(np.float32)
    if cols: v *= np.repeat(np.exp2(rng.integers(-cols, cols + 1, shape[:-2] + (1, shape[-1] // 4))) * (rng.random(shape[:-2] + (1, shape[-1] // 4)) > 0.0625), 4, axis=-1).astype(np.float32)
    return mx_ref.flush(v.astype(BF))
S = 128
def block(rng, how):
    if how == "one": return np.full((8, S), rng.integers(0, 128))
    if how == "groups": return np.tile(rng.integers(0, 128, S), (8, 1))
    if how == "ends": return np.stack([rng.permutation(np.arange(S) % 2 * 127) for g in range(8)])
    if how == "distinct": return np.stack([np.tile(rng.permutation(128), S // 128) for g in range(8)])
    return rng.integers(0, 128, (8, S))
def lists(rng, how=""):
    return {"cw": np.stack([gtable(np.concatenate([block(rng, how) for s in range(N)], axis=1)) for r in range(N)])}
def setup_inputs(rng):
    return {"bk": f(rng, N, 128, 512), "x": f(rng, N, 128, 512 * N), **lists(rng)}
def setup_inputs_one(rng):
    return {**setup_inputs(rng), **lists(rng, "one")}
def setup_inputs_groups(rng):
    return {**setup_inputs(rng), **lists(rng, "groups")}
def setup_inputs_ends(rng):
    return {**setup_inputs(rng), **lists(rng, "ends")}
def setup_inputs_distinct(rng):
    return {**setup_inputs(rng), **lists(rng, "distinct")}
def setup_inputs_spread(rng):
    d = setup_inputs(rng); d["bk"] = wide(rng, N, 128, 512, cols=4); d["x"] = wide(rng, N, 128, 512 * N); return d
def check_inputs(d):
    b = []
    for r in range(N):
        e = d["cw"][r]
        if e.min() < 0 or e.max() > 127: b.append("cw")
    return b
def reference(bk, x, cw):
    y = np.zeros((N, 128, S), np.float32)
    for r in range(N):
        e = gentries(cw[r])
        for s in range(N):
            W = gcols(bk[s], e[:, S * s:S * s + S])
            X = np.ascontiguousarray(x[r][:, 512 * s:512 * s + 512])
            y[r] += mx_ref.matmul(mx_ref.quantize(X), mx_ref.quantize(W))
    return {"y": y}

@@ -1,0 +1,203 @@
+from concourse.bass import DstId, RemoteDMATransfer
+from concourse.mybir import dt, ActivationFunctionType
+
+N = 6
+S = 128
+L = S // 16
+
+SCRATCH = {
+    "cwi": ("sbuf", [128, N * L], "int32"),
+    "lu": ("sbuf", [128, N * L], "uint16"),
+    "off": ("sbuf", [128, (N - 1) * L], "uint16"),
+    "bks": ("sbuf", [128, 4 * S], "bfloat16"),
+    "win": ("sbuf", [128, 4 * S], "bfloat16"),
+    "h": ("sbuf", [128, 4 * S * (N - 1)], "bfloat16"),
+    "ho": ("sbuf", [128, 4 * S], "bfloat16"),
+    "xs": ("sbuf", [128, 4 * S * N], "bfloat16"),
+    "sq": ("sbuf", [128, S * (N - 1)], "float8_e4m3fn_x4"),
+    "ss": ("sbuf", [128, S * (N - 1)], "uint8"),
+    "oq": ("sbuf", [128, S], "float8_e4m3fn_x4"),
+    "osc": ("sbuf", [128, S], "uint8"),
+    "rq": ("sbuf", [128, S * N], "float8_e4m3fn_x4"),
+    "rs": ("sbuf", [128, S * N], "uint8"),
+    "xq": ("sbuf", [128, S * N], "float8_e4m3fn_x4"),
+    "xsc": ("sbuf", [128, S * N], "uint8"),
+    "yo": ("sbuf", [128, S], "float32"),
+    "ps": ("psum", [128, 512], "float32"),
+}
+SEMAPHORES = (["ld_cw", "ld_bk", "ld_x", "cast", "go", "winv", "wins", "ownv", "owns", "ownq", "xqd", "mm", "yc", "st", "sent"]
+              + ["lst%d" % k for k in range(N)] + ["arr%d" % k for k in range(N)]
+              + ["gv%d" % k for k in range(N)] + ["gs%d" % k for k in range(N)] + ["qd%d" % k for k in range(N)])
+
+
+def groups_of(T, topo, s):
+    c = T.cores[s]
+    ring = [(s + d) % N for d in range(1, N)]
+    near = [r for r in ring if topo.die(T.cores[r]) == topo.die(c)]
+    far = [r for r in ring if topo.die(T.cores[r]) != topo.die(c)]
+    if s % 2:
+        far = far[len(far) // 2:] + far[:len(far) // 2]
+    out = []
+    while far:
+        a = far.pop(0)
+        if len(near) > len(far) and near:
+            out.append([a, near.pop(0)])
+        elif far:
+            out.append([a, far.pop(0)])
+        else:
+            out.append([a])
+    while near:
+        out.append(near[:2])
+        near = near[2:]
+    return out
+
+
+def split(engs, k):
+    if k == 3:
+        return [engs[0::4], engs[2::4], engs[1::2]]
+    return [engs[i::k] for i in range(k)]
+
+
+def bits(es):
+    m = 0
+    for e in es:
+        m |= 1 << e
+    return m
+
+
+def rank_program(g, core, T, topo):
+    rank = T.rank_of(core)
+    if rank is None:
+        return
+    cores = T.cores
+    sem = T.sem
+    v, a, te, sy = g.vector, g.scalar, g.tensor, g.sync
+    COPY = ActivationFunctionType.Copy
+
+    groups = [groups_of(T, topo, s) for s in range(N)]
+    order = [[r for grp in groups[s] for r in grp] for s in range(N)]
+    mine = groups[rank]
+
+    def dst(r):
+        rid, pid, _ = topo.addr(cores[r])
+        return DstId(rid=rid, pnc=pid)
+
+    def servers(r):
+        return [s for _, s in sorted((order[s].index(r), s) for s in range(N) if s != r)]
+
+    def list_calls(r):
+        q = servers(r)
+        return [q[:2], q[2:]]
+
+    engs = topo.engines(core, cores[mine[0][0]])
+
+    def list_count(r, s):
+        for call in list_calls(r):
+            if s in call:
+                return len(split(engs, len(call))[call.index(s)])
+
+    left = [0]
+
+    def fused(parts):
+        tr = []
+        for r, src, dv, sm, es in parts:
+            tr.append(RemoteDMATransfer(dst_ids=[dst(r)], dma_engine_mask=bits(es), remote_sem=sm, src=src, dst=dv))
+            left[0] += len(es)
+        g.remote_dma_fused(tr, local_sem=sem.sent)
+
+    sy.dma_start(T.cwi[:], T.cw[:]).then_inc(sem.ld_cw, 16)
+    a.dma_start(T.bks[:], T.bk[:]).then_inc(sem.ld_bk, 16)
+    sy.wait_ge(sem.go, 1)
+    sy.dma_start(T.xs[:], T.x[:]).then_inc(sem.ld_x, 16)
+
+    v.wait_ge(sem.ld_cw, 16)
+    v.tensor_copy(T.lu[:], T.cwi[:]).then_inc(sem.cast, 1)
+    g.wait_ge(sem.cast, 1)
+    for call in list_calls(rank):
+        es = split(engs, len(call))
+        parts = []
+        for i, s in enumerate(call):
+            k = order[s].index(rank)
+            parts.append((s, T.lu[:, L * s:L * s + L], T.off[:, L * k:L * k + L], sem["lst%d" % k], es[i]))
+        fused(parts)
+    g.sem_inc(sem.go, 1)
+
+    def copy(q, o, i, sm):
+        if q is v:
+            v.tensor_copy(o, i).then_inc(sm, 1)
+        else:
+            a.activation(o, i, COPY).then_inc(sm, 1)
+
+    both = ((v, (0, 1)), (a, (2, 3)))
+    for q, ts in both:
+        q.wait_ge(sem.ld_bk, 16)
+        for t in ts:
+            copy(q, T.win[:, S * t:S * t + S], T.bks[:, t:4 * S:4], sem.winv if q is v else sem.wins)
+
+    def gather(q, t, buf, c0, n, offs, sm):
+        copy(q, buf[:, 4 * c0 + t:4 * (c0 + n):4], T.win[:, S * t:S * t + S].indirect(offs), sm)
+
+    own = T.lu[:, L * rank:L * rank + L]
+    v.wait_ge(sem.winv, 2)
+    v.wait_ge(sem.cast, 1)
+    a.wait_ge(sem.wins, 2)
+    a.wait_ge(sem.cast, 1)
+    for q, ts in both:
+        for t in ts:
+            gather(q, t, T.ho, 0, S, own, sem.ownv if q is v else sem.owns)
+    v.wait_ge(sem.ownv, 2)
+    v.wait_ge(sem.owns, 2)
+    v.quantize_mx(T.oq[:], T.osc[:], T.ho[:]).then_inc(sem.ownq, 1)
+
+    k0 = 0
+    for i, grp in enumerate(mine):
+        n = S * len(grp)
+        offs = T.off[:, L * k0:L * (k0 + len(grp))]
+        gv, gs, qd = sem["gv%d" % i], sem["gs%d" % i], sem["qd%d" % i]
+        for q, ts in both:
+            for j, r in enumerate(grp):
+                q.wait_ge(sem["lst%d" % (k0 + j)], list_count(r, rank))
+            for t in ts:
+                gather(q, t, T.h, S * k0, n, offs, gv if q is v else gs)
+        v.wait_ge(gv, 2)
+        v.wait_ge(gs, 2)
+        c0, c1 = S * k0, S * k0 + n
+        v.quantize_mx(T.sq[:, c0:c1], T.ss[:, c0:c1], T.h[:, 4 * c0:4 * c1]).then_inc(qd, 1)
+        g.wait_ge(qd, 1)
+        es = split(engs, len(grp))
+        d0, d1 = S * rank, S * rank + S
+        parts = ([], [])
+        for j, r in enumerate(grp):
+            b0, b1 = S * (k0 + j), S * (k0 + j + 1)
+            sm = sem["arr%d" % rank]
+            parts[0].append((r, T.sq[:, b0:b1].bitcast(dt.uint8), T.rq[:, d0:d1].bitcast(dt.uint8), sm, es[j]))
+            parts[1].append((r, T.ss[:, b0:b1], T.rs[:, d0:d1], sm, es[j]))
+        fused(parts[0])
+        fused(parts[1])
+        k0 += len(grp)
+
+    v.wait_ge(sem.ld_x, 16)
+    half = S * N // 2
+    for i in range(2):
+        b0, b1 = half * i, half * (i + 1)
+        v.quantize_mx(T.xq[:, b0:b1], T.xsc[:, b0:b1], T.xs[:, 4 * b0:4 * b1]).then_inc(sem.xqd, 1)
+
+    def tile(b, s):
+        return b[:, S * s:S * s + S]
+
+    te.wait_ge(sem.xqd, 2)
+    te.wait_ge(sem.ownq, 1)
+    te.matmul_mx(T.ps[:, 0:S], tile(T.xq, rank), tile(T.xsc, rank), T.oq[:], T.osc[:], True, False)
+    for i, s in enumerate(servers(rank)):
+        for grp in groups[s]:
+            if rank in grp:
+                te.wait_ge(sem["arr%d" % s], 2 * len(split(engs, len(grp))[grp.index(rank)]))
+        mm = te.matmul_mx(T.ps[:, 0:S], tile(T.xq, s), tile(T.xsc, s), tile(T.rq, s), tile(T.rs, s), False, i == N - 2)
+        if i == N - 2:
+            mm.then_inc(sem.mm, 1)
+    v.wait_ge(sem.mm, 1)
+    v.tensor_copy(T.yo[:], T.ps[:, 0:S]).then_inc(sem.yc, 1)
+    sy.wait_ge(sem.yc, 1)
+    sy.dma_start(T.y[:], T.yo[:]).then_inc(sem.st, 16)
+    sy.wait_ge(sem.st, 16)
+    g.wait_ge(sem.sent, left[0])

@@ -4,6 +4,7 @@ from concourse.mybir import dt, ActivationFunctionType
 N = 6
 S = 128
 L = S // 16
+CFG = dict(xl=[2, 4], xq=[2, 2, 2], nl=1, nq=1, vs=[2, 2, 1], lc=[2, 2, 1], go=1)
 
 SCRATCH = {
     "cwi": ("sbuf", [128, N * L], "int32"),
@@ -25,7 +26,8 @@ SCRATCH = {
     "yo": ("sbuf", [128, S], "float32"),
     "ps": ("psum", [128, 512], "float32"),
 }
-SEMAPHORES = (["ld_cw", "ld_bk", "ld_x", "cast", "go", "winv", "wins", "ownv", "owns", "ownq", "xqd", "mm", "yc", "st", "sent"]
+SEMAPHORES = (["ld_cw", "ld_bk", "cast", "go", "winv", "wins", "ownv", "owns", "ownq", "mm", "yc", "st", "sent"]
+              + ["ld_x%d" % k for k in range(N)] + ["xqd%d" % k for k in range(N)]
               + ["lst%d" % k for k in range(N)] + ["arr%d" % k for k in range(N)]
               + ["gv%d" % k for k in range(N)] + ["gs%d" % k for k in range(N)] + ["qd%d" % k for k in range(N)])
 
@@ -65,6 +67,10 @@ def bits(es):
     return m
 
 
+def edges(ns):
+    return [(sum(ns[:i]), sum(ns[:i + 1])) for i in range(len(ns))]
+
+
 def rank_program(g, core, T, topo):
     rank = T.rank_of(core)
     if rank is None:
@@ -87,7 +93,7 @@ def rank_program(g, core, T, topo):
 
     def list_calls(r):
         q = servers(r)
-        return [q[:2], q[2:]]
+        return [q[i:j] for i, j in edges(CFG["lc"])]
 
     engs = topo.engines(core, cores[mine[0][0]])
 
@@ -105,22 +111,32 @@ def rank_program(g, core, T, topo):
             left[0] += len(es)
         g.remote_dma_fused(tr, local_sem=sem.sent)
 
+    xl, xq = edges(CFG["xl"]), edges(CFG["xq"])
+
+    def load_x(i):
+        b0, b1 = 4 * S * xl[i][0], 4 * S * xl[i][1]
+        sy.dma_start(T.xs[:, b0:b1], T.x[:, b0:b1]).then_inc(sem["ld_x%d" % i], 16)
+
     sy.dma_start(T.cwi[:], T.cw[:]).then_inc(sem.ld_cw, 16)
-    a.dma_start(T.bks[:], T.bk[:]).then_inc(sem.ld_bk, 16)
+    sy.dma_start(T.bks[:], T.bk[:]).then_inc(sem.ld_bk, 16)
+    for i in range(CFG["nl"]):
+        load_x(i)
     sy.wait_ge(sem.go, 1)
-    sy.dma_start(T.xs[:], T.x[:]).then_inc(sem.ld_x, 16)
+    for i in range(CFG["nl"], len(xl)):
+        load_x(i)
 
     v.wait_ge(sem.ld_cw, 16)
     v.tensor_copy(T.lu[:], T.cwi[:]).then_inc(sem.cast, 1)
     g.wait_ge(sem.cast, 1)
-    for call in list_calls(rank):
+    for c, call in enumerate(list_calls(rank)):
         es = split(engs, len(call))
         parts = []
         for i, s in enumerate(call):
             k = order[s].index(rank)
             parts.append((s, T.lu[:, L * s:L * s + L], T.off[:, L * k:L * k + L], sem["lst%d" % k], es[i]))
         fused(parts)
-    g.sem_inc(sem.go, 1)
+        if c == CFG["go"]:
+            g.sem_inc(sem.go, 1)
 
     def copy(q, o, i, sm):
         if q is v:
@@ -128,8 +144,10 @@ def rank_program(g, core, T, topo):
         else:
             a.activation(o, i, COPY).then_inc(sm, 1)
 
-    both = ((v, (0, 1)), (a, (2, 3)))
-    for q, ts in both:
+    def both(nv):
+        return ((v, range(nv)), (a, range(nv, 4)))
+
+    for q, ts in both(2):
         q.wait_ge(sem.ld_bk, 16)
         for t in ts:
             copy(q, T.win[:, S * t:S * t + S], T.bks[:, t:4 * S:4], sem.winv if q is v else sem.wins)
@@ -142,25 +160,38 @@ def rank_program(g, core, T, topo):
     v.wait_ge(sem.cast, 1)
     a.wait_ge(sem.wins, 2)
     a.wait_ge(sem.cast, 1)
-    for q, ts in both:
+    for q, ts in both(2):
         for t in ts:
             gather(q, t, T.ho, 0, S, own, sem.ownv if q is v else sem.owns)
     v.wait_ge(sem.ownv, 2)
     v.wait_ge(sem.owns, 2)
     v.quantize_mx(T.oq[:], T.osc[:], T.ho[:]).then_inc(sem.ownq, 1)
 
+    def quant_x(i):
+        for k in range(len(xl)):
+            if xl[k][0] < xq[i][1] and xq[i][0] < xl[k][1]:
+                v.wait_ge(sem["ld_x%d" % k], 16)
+        b0, b1 = S * xq[i][0], S * xq[i][1]
+        v.quantize_mx(T.xq[:, b0:b1], T.xsc[:, b0:b1], T.xs[:, 4 * b0:4 * b1]).then_inc(sem["xqd%d" % i], 1)
+
+    for i in range(CFG["nq"]):
+        quant_x(i)
+
+    a.wait_ge(sem.winv, 2)
+    v.wait_ge(sem.wins, 2)
     k0 = 0
     for i, grp in enumerate(mine):
         n = S * len(grp)
+        nv = CFG["vs"][i]
         offs = T.off[:, L * k0:L * (k0 + len(grp))]
         gv, gs, qd = sem["gv%d" % i], sem["gs%d" % i], sem["qd%d" % i]
-        for q, ts in both:
+        for q, ts in both(nv):
             for j, r in enumerate(grp):
                 q.wait_ge(sem["lst%d" % (k0 + j)], list_count(r, rank))
             for t in ts:
                 gather(q, t, T.h, S * k0, n, offs, gv if q is v else gs)
-        v.wait_ge(gv, 2)
-        v.wait_ge(gs, 2)
+        v.wait_ge(gv, nv)
+        v.wait_ge(gs, 4 - nv)
         c0, c1 = S * k0, S * k0 + n
         v.quantize_mx(T.sq[:, c0:c1], T.ss[:, c0:c1], T.h[:, 4 * c0:4 * c1]).then_inc(qd, 1)
         g.wait_ge(qd, 1)
@@ -176,24 +207,30 @@ def rank_program(g, core, T, topo):
         fused(parts[1])
         k0 += len(grp)
 
-    v.wait_ge(sem.ld_x, 16)
-    half = S * N // 2
-    for i in range(2):
-        b0, b1 = half * i, half * (i + 1)
-        v.quantize_mx(T.xq[:, b0:b1], T.xsc[:, b0:b1], T.xs[:, 4 * b0:4 * b1]).then_inc(sem.xqd, 1)
+    for i in range(CFG["nq"], len(xq)):
+        quant_x(i)
 
     def tile(b, s):
         return b[:, S * s:S * s + S]
 
-    te.wait_ge(sem.xqd, 2)
-    te.wait_ge(sem.ownq, 1)
-    te.matmul_mx(T.ps[:, 0:S], tile(T.xq, rank), tile(T.xsc, rank), T.oq[:], T.osc[:], True, False)
-    for i, s in enumerate(servers(rank)):
-        for grp in groups[s]:
-            if rank in grp:
-                te.wait_ge(sem["arr%d" % s], 2 * len(split(engs, len(grp))[grp.index(rank)]))
-        mm = te.matmul_mx(T.ps[:, 0:S], tile(T.xq, s), tile(T.xsc, s), tile(T.rq, s), tile(T.rs, s), False, i == N - 2)
-        if i == N - 2:
+    def part(s):
+        return [p <= s < q for p, q in xq].index(True)
+
+    def arrival(s):
+        return [rank in grp for grp in groups[s]].index(True) if s != rank else 0
+
+    seq = sorted(range(N), key=lambda s: (arrival(s), part(s)))
+    for i, s in enumerate(seq):
+        te.wait_ge(sem["xqd%d" % part(s)], 1)
+        if s == rank:
+            te.wait_ge(sem.ownq, 1)
+            w, ws = T.oq[:], T.osc[:]
+        else:
+            grp = groups[s][arrival(s)]
+            te.wait_ge(sem["arr%d" % s], 2 * len(split(engs, len(grp))[grp.index(rank)]))
+            w, ws = tile(T.rq, s), tile(T.rs, s)
+        mm = te.matmul_mx(T.ps[:, 0:S], tile(T.xq, s), tile(T.xsc, s), w, ws, i == 0, i == N - 1)
+        if i == N - 1:
             mm.then_inc(sem.mm, 1)
     v.wait_ge(sem.mm, 1)
     v.tensor_copy(T.yo[:], T.ps[:, 0:S]).then_inc(sem.yc, 1)

@@ -4,7 +4,9 @@ from concourse.mybir import dt, ActivationFunctionType
 N = 6
 S = 128
 L = S // 16
-CFG = dict(xl=[2, 4], xq=[2, 2, 2], nl=1, nq=1, vs=[2, 2, 1], lc=[2, 2, 1], go=1)
+CFG = dict(cols=[(2, 0), (1, 0), (2, 1), (1, 1), (0, 1)], rounds=[1, 2, 1, 1], vs=[2, 2, 2, 1], ahead=[1, 0, 0, 0],
+           sends=[1, 1, 1, 1, 1], sc=[[0], [], [1, 2], [3], [4]], lc=[1, 2, 2], e1=8, xl=[3, 3], xq=[2, 2, 2], nl=1, nq=1,
+           go=2)
 
 SCRATCH = {
     "cwi": ("sbuf", [128, N * L], "int32"),
@@ -32,26 +34,12 @@ SEMAPHORES = (["ld_cw", "ld_bk", "cast", "go", "winv", "wins", "ownv", "owns", "
               + ["gv%d" % k for k in range(N)] + ["gs%d" % k for k in range(N)] + ["qd%d" % k for k in range(N)])
 
 
-def groups_of(T, topo, s):
-    c = T.cores[s]
-    ring = [(s + d) % N for d in range(1, N)]
-    near = [r for r in ring if topo.die(T.cores[r]) == topo.die(c)]
-    far = [r for r in ring if topo.die(T.cores[r]) != topo.die(c)]
-    if s % 2:
-        far = far[len(far) // 2:] + far[:len(far) // 2]
-    out = []
-    while far:
-        a = far.pop(0)
-        if len(near) > len(far) and near:
-            out.append([a, near.pop(0)])
-        elif far:
-            out.append([a, far.pop(0)])
-        else:
-            out.append([a])
-    while near:
-        out.append(near[:2])
-        near = near[2:]
-    return out
+def edges(ns):
+    return [(sum(ns[:i]), sum(ns[:i + 1])) for i in range(len(ns))]
+
+
+def serves(s):
+    return [2 * ((s // 2 + d) % (N // 2)) + (s + f) % 2 for d, f in CFG["cols"]]
 
 
 def split(engs, k):
@@ -67,10 +55,6 @@ def bits(es):
     return m
 
 
-def edges(ns):
-    return [(sum(ns[:i]), sum(ns[:i + 1])) for i in range(len(ns))]
-
-
 def rank_program(g, core, T, topo):
     rank = T.rank_of(core)
     if rank is None:
@@ -80,27 +64,31 @@ def rank_program(g, core, T, topo):
     v, a, te, sy = g.vector, g.scalar, g.tensor, g.sync
     COPY = ActivationFunctionType.Copy
 
-    groups = [groups_of(T, topo, s) for s in range(N)]
-    order = [[r for grp in groups[s] for r in grp] for s in range(N)]
-    mine = groups[rank]
+    rounds, sends, lists = edges(CFG["rounds"]), edges(CFG["sends"]), edges(CFG["lc"])
+    codes, scales = [list(range(i, j)) for i, j in sends], CFG["sc"]
+    xl, xq = edges(CFG["xl"]), edges(CFG["xq"])
+    mine = serves(rank)
 
     def dst(r):
         rid, pid, _ = topo.addr(cores[r])
         return DstId(rid=rid, pnc=pid)
 
-    def servers(r):
-        return [s for _, s in sorted((order[s].index(r), s) for s in range(N) if s != r)]
+    def place(s, r):
+        return serves(s).index(r)
 
-    def list_calls(r):
-        q = servers(r)
-        return [q[i:j] for i, j in edges(CFG["lc"])]
+    servers = sorted([s for s in range(N) if s != rank], key=lambda s: place(s, rank))
+    engs = topo.engines(core, cores[mine[0]])
 
-    engs = topo.engines(core, cores[mine[0][0]])
+    def list_engs(c, n):
+        return split(engs[::len(engs) // CFG["e1"]] if c == 0 else engs, n)
 
-    def list_count(r, s):
-        for call in list_calls(r):
-            if s in call:
-                return len(split(engs, len(call))[call.index(s)])
+    def list_count(k):
+        for c, (i, j) in enumerate(lists):
+            if i <= k < j:
+                return len(list_engs(c, j - i)[k - i])
+
+    def arr_count(k):
+        return sum(len(split(engs, len(ks))[ks.index(k)]) for ks in codes + scales if k in ks)
 
     left = [0]
 
@@ -110,8 +98,6 @@ def rank_program(g, core, T, topo):
             tr.append(RemoteDMATransfer(dst_ids=[dst(r)], dma_engine_mask=bits(es), remote_sem=sm, src=src, dst=dv))
             left[0] += len(es)
         g.remote_dma_fused(tr, local_sem=sem.sent)
-
-    xl, xq = edges(CFG["xl"]), edges(CFG["xq"])
 
     def load_x(i):
         b0, b1 = 4 * S * xl[i][0], 4 * S * xl[i][1]
@@ -128,12 +114,12 @@ def rank_program(g, core, T, topo):
     v.wait_ge(sem.ld_cw, 16)
     v.tensor_copy(T.lu[:], T.cwi[:]).then_inc(sem.cast, 1)
     g.wait_ge(sem.cast, 1)
-    for c, call in enumerate(list_calls(rank)):
-        es = split(engs, len(call))
+    for c, (i, j) in enumerate(lists):
+        es = list_engs(c, j - i)
         parts = []
-        for i, s in enumerate(call):
-            k = order[s].index(rank)
-            parts.append((s, T.lu[:, L * s:L * s + L], T.off[:, L * k:L * k + L], sem["lst%d" % k], es[i]))
+        for k in range(i, j):
+            s = servers[k]
+            parts.append((s, T.lu[:, L * s:L * s + L], T.off[:, L * k:L * k + L], sem["lst%d" % k], es[k - i]))
         fused(parts)
         if c == CFG["go"]:
             g.sem_inc(sem.go, 1)
@@ -144,10 +130,8 @@ def rank_program(g, core, T, topo):
         else:
             a.activation(o, i, COPY).then_inc(sm, 1)
 
-    def both(nv):
-        return ((v, range(nv)), (a, range(nv, 4)))
-
-    for q, ts in both(2):
+    both = ((v, (0, 1)), (a, (2, 3)))
+    for q, ts in both:
         q.wait_ge(sem.ld_bk, 16)
         for t in ts:
             copy(q, T.win[:, S * t:S * t + S], T.bks[:, t:4 * S:4], sem.winv if q is v else sem.wins)
@@ -160,7 +144,7 @@ def rank_program(g, core, T, topo):
     v.wait_ge(sem.cast, 1)
     a.wait_ge(sem.wins, 2)
     a.wait_ge(sem.cast, 1)
-    for q, ts in both(2):
+    for q, ts in both:
         for t in ts:
             gather(q, t, T.ho, 0, S, own, sem.ownv if q is v else sem.owns)
     v.wait_ge(sem.ownv, 2)
@@ -177,35 +161,45 @@ def rank_program(g, core, T, topo):
     for i in range(CFG["nq"]):
         quant_x(i)
 
+    def copies(q, i, ts):
+        k0, k1 = rounds[i]
+        for k in range(k0, k1):
+            q.wait_ge(sem["lst%d" % k], list_count(k))
+        for t in ts:
+            gather(q, t, T.h, S * k0, S * (k1 - k0), T.off[:, L * k0:L * k1], sem["gv%d" % i] if q is v else sem["gs%d" % i])
+
+    def send(ks, src, dv, coded):
+        es = split(engs, len(ks))
+        parts = []
+        for e, k in zip(es, ks):
+            x, z = src[:, S * k:S * k + S], dv[:, S * rank:S * rank + S]
+            if coded:
+                x, z = x.bitcast(dt.uint8), z.bitcast(dt.uint8)
+            parts.append((mine[k], x, z, sem["arr%d" % rank], e))
+        fused(parts)
+
     a.wait_ge(sem.winv, 2)
     v.wait_ge(sem.wins, 2)
-    k0 = 0
-    for i, grp in enumerate(mine):
-        n = S * len(grp)
+    begun = 0
+    for i, (k0, k1) in enumerate(rounds):
         nv = CFG["vs"][i]
-        offs = T.off[:, L * k0:L * (k0 + len(grp))]
-        gv, gs, qd = sem["gv%d" % i], sem["gs%d" % i], sem["qd%d" % i]
-        for q, ts in both(nv):
-            for j, r in enumerate(grp):
-                q.wait_ge(sem["lst%d" % (k0 + j)], list_count(r, rank))
-            for t in ts:
-                gather(q, t, T.h, S * k0, n, offs, gv if q is v else gs)
-        v.wait_ge(gv, nv)
-        v.wait_ge(gs, 4 - nv)
-        c0, c1 = S * k0, S * k0 + n
-        v.quantize_mx(T.sq[:, c0:c1], T.ss[:, c0:c1], T.h[:, 4 * c0:4 * c1]).then_inc(qd, 1)
-        g.wait_ge(qd, 1)
-        es = split(engs, len(grp))
-        d0, d1 = S * rank, S * rank + S
-        parts = ([], [])
-        for j, r in enumerate(grp):
-            b0, b1 = S * (k0 + j), S * (k0 + j + 1)
-            sm = sem["arr%d" % rank]
-            parts[0].append((r, T.sq[:, b0:b1].bitcast(dt.uint8), T.rq[:, d0:d1].bitcast(dt.uint8), sm, es[j]))
-            parts[1].append((r, T.ss[:, b0:b1], T.rs[:, d0:d1], sm, es[j]))
-        fused(parts[0])
-        fused(parts[1])
-        k0 += len(grp)
+        copies(a, i, range(nv, 4))
+        copies(v, i, range(begun, nv))
+        begun = CFG["ahead"][i]
+        if begun:
+            copies(v, i + 1, range(begun))
+        v.wait_ge(sem["gv%d" % i], nv)
+        v.wait_ge(sem["gs%d" % i], 4 - nv)
+        for m, (j0, j1) in enumerate(sends):
+            if not k0 <= j0 < k1:
+                continue
+            qd = sem["qd%d" % m]
+            c0, c1 = S * j0, S * j1
+            v.quantize_mx(T.sq[:, c0:c1], T.ss[:, c0:c1], T.h[:, 4 * c0:4 * c1]).then_inc(qd, 1)
+            g.wait_ge(qd, 1)
+            send(codes[m], T.sq, T.rq, True)
+            if scales[m]:
+                send(scales[m], T.ss, T.rs, False)
 
     for i in range(CFG["nq"], len(xq)):
         quant_x(i)
@@ -217,7 +211,7 @@ def rank_program(g, core, T, topo):
         return [p <= s < q for p, q in xq].index(True)
 
     def arrival(s):
-        return [rank in grp for grp in groups[s]].index(True) if s != rank else 0
+        return [place(s, rank) in ks for ks in scales].index(True) if s != rank else 0
 
     seq = sorted(range(N), key=lambda s: (arrival(s), part(s)))
     for i, s in enumerate(seq):
@@ -226,15 +220,15 @@ def rank_program(g, core, T, topo):
             te.wait_ge(sem.ownq, 1)
             w, ws = T.oq[:], T.osc[:]
         else:
-            grp = groups[s][arrival(s)]
-            te.wait_ge(sem["arr%d" % s], 2 * len(split(engs, len(grp))[grp.index(rank)]))
+            te.wait_ge(sem["arr%d" % s], arr_count(place(s, rank)))
             w, ws = tile(T.rq, s), tile(T.rs, s)
         mm = te.matmul_mx(T.ps[:, 0:S], tile(T.xq, s), tile(T.xsc, s), w, ws, i == 0, i == N - 1)
         if i == N - 1:
             mm.then_inc(sem.mm, 1)
-    v.wait_ge(sem.mm, 1)
-    v.tensor_copy(T.yo[:], T.ps[:, 0:S]).then_inc(sem.yc, 1)
-    sy.wait_ge(sem.yc, 1)
-    sy.dma_start(T.y[:], T.yo[:]).then_inc(sem.st, 16)
-    sy.wait_ge(sem.st, 16)
+
+    a.wait_ge(sem.mm, 1)
+    a.activation(T.yo[:], T.ps[:, 0:S], COPY).then_inc(sem.yc, 1)
+    a.wait_ge(sem.yc, 1)
+    a.dma_start(T.y[:], T.yo[:]).then_inc(sem.st, 16)
+    a.wait_ge(sem.st, 16)
     g.wait_ge(sem.sent, left[0])

from concourse.bass import DstId, RemoteDMATransfer
from concourse.mybir import dt, ActivationFunctionType

N = 6
S = 128
L = S // 16
CFG = dict(cols=[(2, 0), (1, 0), (2, 1), (1, 1), (0, 1)], rounds=[1, 2, 1, 1], vs=[2, 2, 2, 1], ahead=[1, 0, 0, 0],
           sends=[1, 1, 1, 1, 1], sc=[[0], [], [1, 2], [3], [4]], lc=[1, 2, 2], e1=8, xl=[3, 3], xq=[2, 2, 2], nl=1, nq=1,
           go=2)

SCRATCH = {
    "cwi": ("sbuf", [128, N * L], "int32"),
    "lu": ("sbuf", [128, N * L], "uint16"),
    "off": ("sbuf", [128, (N - 1) * L], "uint16"),
    "bks": ("sbuf", [128, 4 * S], "bfloat16"),
    "win": ("sbuf", [128, 4 * S], "bfloat16"),
    "h": ("sbuf", [128, 4 * S * (N - 1)], "bfloat16"),
    "ho": ("sbuf", [128, 4 * S], "bfloat16"),
    "xs": ("sbuf", [128, 4 * S * N], "bfloat16"),
    "sq": ("sbuf", [128, S * (N - 1)], "float8_e4m3fn_x4"),
    "ss": ("sbuf", [128, S * (N - 1)], "uint8"),
    "oq": ("sbuf", [128, S], "float8_e4m3fn_x4"),
    "osc": ("sbuf", [128, S], "uint8"),
    "rq": ("sbuf", [128, S * N], "float8_e4m3fn_x4"),
    "rs": ("sbuf", [128, S * N], "uint8"),
    "xq": ("sbuf", [128, S * N], "float8_e4m3fn_x4"),
    "xsc": ("sbuf", [128, S * N], "uint8"),
    "yo": ("sbuf", [128, S], "float32"),
    "ps": ("psum", [128, 512], "float32"),
}
SEMAPHORES = (["ld_cw", "ld_bk", "cast", "go", "winv", "wins", "ownv", "owns", "ownq", "mm", "yc", "st", "sent"]
              + ["ld_x%d" % k for k in range(N)] + ["xqd%d" % k for k in range(N)]
              + ["lst%d" % k for k in range(N)] + ["arr%d" % k for k in range(N)]
              + ["gv%d" % k for k in range(N)] + ["gs%d" % k for k in range(N)] + ["qd%d" % k for k in range(N)])


def edges(ns):
    return [(sum(ns[:i]), sum(ns[:i + 1])) for i in range(len(ns))]


def serves(s):
    return [2 * ((s // 2 + d) % (N // 2)) + (s + f) % 2 for d, f in CFG["cols"]]


def split(engs, k):
    if k == 3:
        return [engs[0::4], engs[2::4], engs[1::2]]
    return [engs[i::k] for i in range(k)]


def bits(es):
    m = 0
    for e in es:
        m |= 1 << e
    return m


def rank_program(g, core, T, topo):
    rank = T.rank_of(core)
    if rank is None:
        return
    cores = T.cores
    sem = T.sem
    v, a, te, sy = g.vector, g.scalar, g.tensor, g.sync
    COPY = ActivationFunctionType.Copy

    rounds, sends, lists = edges(CFG["rounds"]), edges(CFG["sends"]), edges(CFG["lc"])
    codes, scales = [list(range(i, j)) for i, j in sends], CFG["sc"]
    xl, xq = edges(CFG["xl"]), edges(CFG["xq"])
    mine = serves(rank)

    def dst(r):
        rid, pid, _ = topo.addr(cores[r])
        return DstId(rid=rid, pnc=pid)

    def place(s, r):
        return serves(s).index(r)

    servers = sorted([s for s in range(N) if s != rank], key=lambda s: place(s, rank))
    engs = topo.engines(core, cores[mine[0]])

    def list_engs(c, n):
        return split(engs[::len(engs) // CFG["e1"]] if c == 0 else engs, n)

    def list_count(k):
        for c, (i, j) in enumerate(lists):
            if i <= k < j:
                return len(list_engs(c, j - i)[k - i])

    def arr_count(k):
        return sum(len(split(engs, len(ks))[ks.index(k)]) for ks in codes + scales if k in ks)

    left = [0]

    def fused(parts):
        tr = []
        for r, src, dv, sm, es in parts:
            tr.append(RemoteDMATransfer(dst_ids=[dst(r)], dma_engine_mask=bits(es), remote_sem=sm, src=src, dst=dv))
            left[0] += len(es)
        g.remote_dma_fused(tr, local_sem=sem.sent)

    def load_x(i):
        b0, b1 = 4 * S * xl[i][0], 4 * S * xl[i][1]
        sy.dma_start(T.xs[:, b0:b1], T.x[:, b0:b1]).then_inc(sem["ld_x%d" % i], 16)

    sy.dma_start(T.cwi[:], T.cw[:]).then_inc(sem.ld_cw, 16)
    sy.dma_start(T.bks[:], T.bk[:]).then_inc(sem.ld_bk, 16)
    for i in range(CFG["nl"]):
        load_x(i)
    sy.wait_ge(sem.go, 1)
    for i in range(CFG["nl"], len(xl)):
        load_x(i)

    v.wait_ge(sem.ld_cw, 16)
    v.tensor_copy(T.lu[:], T.cwi[:]).then_inc(sem.cast, 1)
    g.wait_ge(sem.cast, 1)
    for c, (i, j) in enumerate(lists):
        es = list_engs(c, j - i)
        parts = []
        for k in range(i, j):
            s = servers[k]
            parts.append((s, T.lu[:, L * s:L * s + L], T.off[:, L * k:L * k + L], sem["lst%d" % k], es[k - i]))
        fused(parts)
        if c == CFG["go"]:
            g.sem_inc(sem.go, 1)

    def copy(q, o, i, sm):
        if q is v:
            v.tensor_copy(o, i).then_inc(sm, 1)
        else:
            a.activation(o, i, COPY).then_inc(sm, 1)

    both = ((v, (0, 1)), (a, (2, 3)))
    for q, ts in both:
        q.wait_ge(sem.ld_bk, 16)
        for t in ts:
            copy(q, T.win[:, S * t:S * t + S], T.bks[:, t:4 * S:4], sem.winv if q is v else sem.wins)

    def gather(q, t, buf, c0, n, offs, sm):
        copy(q, buf[:, 4 * c0 + t:4 * (c0 + n):4], T.win[:, S * t:S * t + S].indirect(offs), sm)

    own = T.lu[:, L * rank:L * rank + L]
    v.wait_ge(sem.winv, 2)
    v.wait_ge(sem.cast, 1)
    a.wait_ge(sem.wins, 2)
    a.wait_ge(sem.cast, 1)
    for q, ts in both:
        for t in ts:
            gather(q, t, T.ho, 0, S, own, sem.ownv if q is v else sem.owns)
    v.wait_ge(sem.ownv, 2)
    v.wait_ge(sem.owns, 2)
    v.quantize_mx(T.oq[:], T.osc[:], T.ho[:]).then_inc(sem.ownq, 1)

    def quant_x(i):
        for k in range(len(xl)):
            if xl[k][0] < xq[i][1] and xq[i][0] < xl[k][1]:
                v.wait_ge(sem["ld_x%d" % k], 16)
        b0, b1 = S * xq[i][0], S * xq[i][1]
        v.quantize_mx(T.xq[:, b0:b1], T.xsc[:, b0:b1], T.xs[:, 4 * b0:4 * b1]).then_inc(sem["xqd%d" % i], 1)

    for i in range(CFG["nq"]):
        quant_x(i)

    def copies(q, i, ts):
        k0, k1 = rounds[i]
        for k in range(k0, k1):
            q.wait_ge(sem["lst%d" % k], list_count(k))
        for t in ts:
            gather(q, t, T.h, S * k0, S * (k1 - k0), T.off[:, L * k0:L * k1], sem["gv%d" % i] if q is v else sem["gs%d" % i])

    def send(ks, src, dv, coded):
        es = split(engs, len(ks))
        parts = []
        for e, k in zip(es, ks):
            x, z = src[:, S * k:S * k + S], dv[:, S * rank:S * rank + S]
            if coded:
                x, z = x.bitcast(dt.uint8), z.bitcast(dt.uint8)
            parts.append((mine[k], x, z, sem["arr%d" % rank], e))
        fused(parts)

    a.wait_ge(sem.winv, 2)
    v.wait_ge(sem.wins, 2)
    begun = 0
    for i, (k0, k1) in enumerate(rounds):
        nv = CFG["vs"][i]
        copies(a, i, range(nv, 4))
        copies(v, i, range(begun, nv))
        begun = CFG["ahead"][i]
        if begun:
            copies(v, i + 1, range(begun))
        v.wait_ge(sem["gv%d" % i], nv)
        v.wait_ge(sem["gs%d" % i], 4 - nv)
        for m, (j0, j1) in enumerate(sends):
            if not k0 <= j0 < k1:
                continue
            qd = sem["qd%d" % m]
            c0, c1 = S * j0, S * j1
            v.quantize_mx(T.sq[:, c0:c1], T.ss[:, c0:c1], T.h[:, 4 * c0:4 * c1]).then_inc(qd, 1)
            g.wait_ge(qd, 1)
            send(codes[m], T.sq, T.rq, True)
            if scales[m]:
                send(scales[m], T.ss, T.rs, False)

    for i in range(CFG["nq"], len(xq)):
        quant_x(i)

    def tile(b, s):
        return b[:, S * s:S * s + S]

    def part(s):
        return [p <= s < q for p, q in xq].index(True)

    def arrival(s):
        return [place(s, rank) in ks for ks in scales].index(True) if s != rank else 0

    seq = sorted(range(N), key=lambda s: (arrival(s), part(s)))
    for i, s in enumerate(seq):
        te.wait_ge(sem["xqd%d" % part(s)], 1)
        if s == rank:
            te.wait_ge(sem.ownq, 1)
            w, ws = T.oq[:], T.osc[:]
        else:
            te.wait_ge(sem["arr%d" % s], arr_count(place(s, rank)))
            w, ws = tile(T.rq, s), tile(T.rs, s)
        mm = te.matmul_mx(T.ps[:, 0:S], tile(T.xq, s), tile(T.xsc, s), w, ws, i == 0, i == N - 1)
        if i == N - 1:
            mm.then_inc(sem.mm, 1)

    a.wait_ge(sem.mm, 1)
    a.activation(T.yo[:], T.ps[:, 0:S], COPY).then_inc(sem.yc, 1)
    a.wait_ge(sem.yc, 1)
    a.dma_start(T.y[:], T.yo[:]).then_inc(sem.st, 16)
    a.wait_ge(sem.st, 16)
    g.wait_ge(sem.sent, left[0])
